import numpy as np
import ml_dtypes


def mxq(x, axis, fmt="e4m3"):
    dtype, down = {"e4m3": (ml_dtypes.float8_e4m3fn, 7), "e5m2": (ml_dtypes.float8_e5m2, 14)}[fmt]
    v = np.moveaxis(np.asarray(x, np.float32).astype(ml_dtypes.bfloat16).astype(np.float64), axis, -1)
    blocks = v.reshape(v.shape[:-1] + (-1, 32))
    amax = np.abs(blocks).max(-1, keepdims=True)
    byte = np.maximum(np.where(amax > 0, np.frexp(amax)[1] - 1 + 127, 0) - down, 1)
    scale = np.exp2(byte - 127.0)
    codes = (blocks / scale).astype(np.float32).astype(dtype).astype(np.float64)
    return np.moveaxis((codes * scale).reshape(v.shape), -1, axis)


WIDE = False


def mx_kscale(k):
    if not WIDE:
        return np.ones(k)
    levels = np.array([10, -10, 5, -5, 0])
    if k % 512:
        return np.exp2(np.random.permutation(np.resize(levels, k // 32))).repeat(32)
    a = np.empty((k // 512, 16))
    for p in range(k // 512):
        a[p, :8] = np.random.permutation(np.resize(levels, 8))
        for g in range(8):
            far = levels[np.abs(levels - a[p, g]) >= 10]
            a[p, g + 8] = far[np.random.randint(len(far))]
    return np.exp2(a.ravel()).repeat(32)


def f64(x):
    return np.asarray(x).astype(np.float64)


def striped(idx):
    return np.tile(idx.reshape(-1, 16).T, (8, 1)).astype(np.uint16)


def unstriped(offs):
    return offs[:16].T.reshape(-1).astype(np.int64)


def striped8(idx):
    return np.concatenate([x.reshape(-1, 16).T for x in idx]).astype(np.uint16)


def runs(offs, k):
    lists = np.stack([offs[16 * r : 16 * r + 16].T.reshape(-1) for r in range(8)]).astype(np.int64)
    return lists[np.arange(k) % 512 // 64]


def pack_weight(w):
    k, n = w.shape
    w = f64(np.asarray(w, np.float32).astype(ml_dtypes.bfloat16)).reshape(k // 32, 32, n)
    amax = np.abs(w).max(1)
    byte = np.clip(np.where(amax > 0, np.frexp(amax)[1] - 1 + 127 - 7, 1), 1, 254)
    scaled = (w * np.exp2(127.0 - byte)[:, None, :]).reshape(k, n).astype(np.float32)
    words = np.ascontiguousarray(scaled.reshape(k // 512, 128, 4, n).transpose(0, 1, 3, 2)).astype(ml_dtypes.float8_e4m3fn).view(np.uint8)
    return words, np.ascontiguousarray(byte.astype(np.uint8).reshape(k // 512, 16, n))


def unpack_weight(words, scales):
    g, p, n, _ = words.shape
    vals = np.ascontiguousarray(words).view(ml_dtypes.float8_e4m3fn).astype(np.float64) * np.repeat(np.exp2(scales.astype(np.float64) - 127.0), 8, axis=1)[..., None]
    return vals.transpose(0, 1, 3, 2).reshape(g * 512, n)


K, T, S, N, G, H = 512, 2048, 512, 512, 2048, 512


def setup_inputs():
    n = np.random.standard_normal
    s = mx_kscale(K)[:, None]
    u = mx_kscale(H)
    packed_xT = pack_weight(n((K, T)) * s)
    packed_dT = pack_weight(n((K, G)) / s)
    return {
        "x_words": packed_xT[0],
        "x_scales": packed_xT[1],
        "d_words": packed_dT[0],
        "d_scales": packed_dT[1],
        "gn": (np.random.uniform(0.5, 1.5, (H, 1)) * u[:, None]).astype(np.float32),
        "w1": (n((H, N)) / np.sqrt(H) / u[:, None]).astype(np.float32),
        "offs": striped(np.random.permutation(T)[:S]),
        "kidx": striped8(np.random.randint(0, G, (8, H))),
        "n1": striped8(np.stack([np.random.permutation(S) for _ in range(8)])),
        "n2": striped8(np.stack([np.random.permutation(S) for _ in range(8)])),
    }


def reference(x_words, x_scales, d_words, d_scales, gn, w1, offs, kidx, n1, n2):
    d_kidx = unpack_weight(d_words, d_scales)[np.arange(K)[:, None], runs(kidx, K)]
    xq = unpack_weight(x_words, x_scales)[:, unstriped(offs)]
    s = 0.0625 * (d_kidx.T @ xq)
    a = s[np.arange(H)[:, None], runs(n1, H)]
    b = s[np.arange(H)[:, None], runs(n2, H)]
    mu = 0.3125 * (s + a + b)
    z = f64(gn) * ((s - mu) / (np.sqrt(0.5 * ((a - mu) ** 2 + (b - mu) ** 2) + 0.1)))
    return mxq(f64(w1), 0, "e4m3").T @ mxq(z, 0, "e4m3")

@@ -1,0 +1,215 @@
+from contextlib import ExitStack
+
+import concourse.mybir as mybir
+from concourse.masks import make_identity
+
+F32 = mybir.dt.float32
+BF16 = mybir.dt.bfloat16
+I32 = mybir.dt.int32
+U32 = mybir.dt.uint32
+U16 = mybir.dt.uint16
+U8 = mybir.dt.uint8
+FP8X4 = mybir.dt.float8_e4m3fn_x4
+ALU = mybir.AluOpType
+ACT = mybir.ActivationFunctionType
+
+P = 128
+PACK = 4
+TABLE = 2048
+S = 512
+H = 512
+N = 512
+CHUNK = 128
+CHUNKS = S // CHUNK
+HALF = S // 2
+FLOPS = 2 * 512 * H * S + 2 * H * N * S
+
+
+def tile_picked_scorestd_none_p_kernel(
+    tc, x_words, x_scales, d_words, d_scales, gn, w1, offs, kidx, n1, n2, out
+):
+    nc = tc.nc
+    with ExitStack() as ctx:
+        keep = ctx.enter_context(tc.tile_pool(name="keep", bufs=1))
+        psum = ctx.enter_context(tc.psum_pool(name="psum", bufs=1))
+
+        def bank(shape, tag):
+            return psum.tile(shape, F32, name=tag, tag=tag)
+
+        kidx_sb = keep.tile([P, H // 16], U16, name="kidx_sb")
+        offs_sb = keep.tile([P, S // 16], U16, name="offs_sb")
+        n1_sb = keep.tile([P, S // 16], U16, name="n1_sb")
+        n2_sb = keep.tile([P, S // 16], U16, name="n2_sb")
+        d_bytes = keep.tile([P, TABLE], U8, name="d_bytes")
+        x_bytes = keep.tile([P, TABLE], U8, name="x_bytes")
+        d_table = keep.tile([P, TABLE], U32, name="d_table", tag="big_a")
+        x_table = keep.tile([P, TABLE], U32, name="x_table")
+        gn_sb = keep.tile([P, PACK], F32, name="gn_sb")
+
+        nc.vector.memset(d_bytes[:].bitcast(I32), 0)
+        nc.vector.memset(x_bytes[:].bitcast(I32), 0)
+        nc.sync.dma_start(kidx_sb[:], kidx)
+        nc.sync.dma_start(offs_sb[:], offs)
+        nc.sync.dma_start(out=d_bytes[0:P:8, :].bitcast(I32), in_=d_scales[0].bitcast(I32))
+        nc.sync.dma_start(out=x_bytes[0:P:8, :].bitcast(I32), in_=x_scales[0].bitcast(I32))
+        nc.sync.dma_start(n1_sb[:], n1)
+        nc.sync.dma_start(n2_sb[:], n2)
+        nc.scalar.dma_start(out=gn_sb[:], in_=gn.rearrange("(p t) o -> p (t o)", t=PACK))
+        nc.sync.dma_start(out=d_table[:].bitcast(I32), in_=d_words[0].rearrange("p n t -> p (n t)").bitcast(I32))
+        nc.sync.dma_start(out=x_table[:].bitcast(I32), in_=x_words[0].rearrange("p n t -> p (n t)").bitcast(I32))
+
+        ident = keep.tile([P, P], F32, name="ident")
+        make_identity(nc, ident[:])
+        planes = keep.tile([P, H + S], U8, name="planes", align_bytes=64)
+        nc.vector.memset(planes[:].bitcast(I32), 0)
+
+        warm = keep.tile([P, 1], F32, name="warm")
+        nc.scalar.activation(warm[:], ident[:, 0:1], ACT.Abs_reciprocal_sqrt, bias=1.0)
+
+        d_bytes_picked = keep.tile([P, H], U8, name="d_bytes_picked")
+        x_bytes_picked = keep.tile([P, S], U8, name="x_bytes_picked")
+        staged = keep.tile([P, H + S], U8, name="staged")
+        nc.vector.tensor_copy(d_bytes_picked[:], d_bytes[:].indirect(kidx_sb[:]))
+        nc.vector.tensor_copy(x_bytes_picked[:], x_bytes[:].indirect(offs_sb[:]))
+        nc.vector.tensor_copy(
+            staged[:, 0:H].rearrange("p (t m) -> p m t", t=PACK),
+            d_bytes_picked[:].rearrange("p (m t) -> p m t", t=PACK),
+        )
+        nc.vector.tensor_copy(staged[:, H : H + S].bitcast(I32), x_bytes_picked[:].bitcast(I32))
+        for r in range(4):
+            nc.scalar.dma_start(out=planes[r:P:32, :].bitcast(I32), in_=staged[8 * r : P : 32, :].bitcast(I32))
+
+        d_picked = keep.tile([P, H], U32, name="d_picked")
+        d_dealt = keep.tile([P, H], U32, name="d_dealt", align_bytes=64)
+        nc.vector.tensor_copy(d_picked[:], d_table[:].indirect(kidx_sb[:]))
+        nc.vector.tensor_copy(
+            d_dealt[:].rearrange("p (t m) -> p m t", t=PACK),
+            d_picked[:].rearrange("p (m t) -> p m t", t=PACK),
+        )
+        w_raw = keep.tile([P, PACK, N], F32, name="w_raw", tag="big_a")
+        nc.sync.dma_start(out=w_raw[:], in_=w1.rearrange("(p t) m -> p t m", t=PACK))
+
+        row_scale = keep.tile([P, PACK], F32, name="row_scale")
+        gn_safe = keep.tile([P, PACK], F32, name="gn_safe")
+        gn_inv = keep.tile([P, PACK], F32, name="gn_inv")
+        gn_inv_sq = keep.tile([P, PACK], F32, name="gn_inv_sq")
+        nc.vector.tensor_scalar(row_scale[:], gn_sb[:], 0.0625 * 0.3125 / 0.6, None, ALU.mult)
+        nc.vector.scalar_tensor_tensor(gn_safe[:], gn_sb[:], 0.0, gn_sb[:], ALU.is_equal, ALU.add)
+        nc.vector.reciprocal(gn_inv[:], gn_safe[:])
+        nc.vector.tensor_tensor(gn_inv_sq[:], gn_inv[:], gn_inv[:], ALU.mult)
+
+        x_picked = keep.tile([P, S], U32, name="x_picked", align_bytes=64)
+        scores = [bank([P, S], "product%d" % t) for t in range(PACK)]
+        win = [keep.tile([P, S], F32, name="win%d" % t) for t in range(PACK)]
+        for h in range(2):
+            cols = slice(h * HALF, (h + 1) * HALF)
+            nc.vector.tensor_copy(x_picked[:, cols], x_table[:].indirect(offs_sb[:, h * 16 : (h + 1) * 16]))
+        for t in range(PACK):
+            keys = slice(t * P, (t + 1) * P)
+            for h in range(2):
+                cols = slice(h * HALF, (h + 1) * HALF)
+                nc.tensor.matmul_mx(
+                    out=scores[t][:, cols],
+                    lhsT=d_dealt[:, keys].bitcast(FP8X4),
+                    lhsT_scale=planes[:, keys],
+                    rhs=x_picked[:, cols].bitcast(FP8X4),
+                    rhs_scale=planes[:, H + h * HALF : H + (h + 1) * HALF],
+                    start=True,
+                    stop=True,
+                )
+            nc.scalar.activation(win[t][:], scores[t][:], ACT.Copy, scale=row_scale[:, t : t + 1])
+
+        def add_turned(dst, first, second):
+            nc.tensor.matmul(dst, first, ident[:], start=True, stop=False, is_transpose=True)
+            nc.tensor.matmul(dst, second, ident[:], start=False, stop=True, is_transpose=True)
+
+        both = [keep.tile([P, PACK, HALF], F32, name="both%d" % h) for h in range(2)]
+        inv_root = []
+        for c in range(CHUNKS):
+            cols = slice(c * CHUNK, (c + 1) * CHUNK)
+            entries = slice(c * CHUNK // 16, (c + 1) * CHUNK // 16)
+            a_neg = keep.tile([P, PACK, CHUNK], F32, name="a_neg%d" % c)
+            b_pos = keep.tile([P, PACK, CHUNK], F32, name="b_pos%d" % c)
+            for t in range(PACK):
+                nc.vector.tensor_scalar(a_neg[:, t, :], win[t][:].indirect(n1_sb[:, entries]), -0.6, 0.0, ALU.mult, ALU.add)
+                nc.vector.tensor_scalar(b_pos[:, t, :], win[t][:].indirect(n2_sb[:, entries]), 0.6, 0.0, ALU.mult, ALU.add)
+            u = both[c // 2][:, :, (c % 2) * CHUNK : (c % 2 + 1) * CHUNK]
+            nc.vector.tensor_tensor(u, a_neg[:], b_pos[:], ALU.subtract)
+
+            diff_t = bank([P, PACK, P], "turned%d" % min(c, 1))
+            for t in range(PACK):
+                add_turned(diff_t[:, t, :], a_neg[:, t, :], b_pos[:, t, :])
+            diff_sq = keep.tile([P, PACK, P], F32, name="diff_sq%d" % c)
+            nc.scalar.activation(diff_sq[:], diff_t[:], ACT.Square, scale=1.6)
+            mean_t = bank([P, PACK, P], "turned%d" % (1 - min(c, 1)))
+            for t in range(PACK):
+                add_turned(mean_t[:, t, :], win[t][:, cols], u[:, t, :])
+            mean_sq = keep.tile([P, PACK, P], F32, name="mean_sq%d" % c)
+            nc.scalar.activation(mean_sq[:], mean_t[:], ACT.Square, scale=0.6)
+            spread = bank([P, PACK, CHUNK], "spread%d" % (c % 2))
+            for t in range(PACK):
+                add_turned(spread[:, t, :], diff_sq[:, t, :], mean_sq[:, t, :])
+            r = keep.tile([P, PACK, CHUNK], F32, name="inv_root%d" % c)
+            for t in range(PACK):
+                nc.scalar.activation(
+                    r[:, t, :], spread[:, t, :], ACT.Abs_reciprocal_sqrt, bias=0.1, scale=gn_inv_sq[:, t : t + 1]
+                )
+            inv_root.append(r)
+
+            if c == 0:
+                w_bf = keep.tile([P, N, PACK], BF16, name="w_bf", align_bytes=64)
+                for mb in range(N // P):
+                    rows = slice(mb * P, (mb + 1) * P)
+                    nc.scalar.copy(
+                        w_bf[:, rows, :].rearrange("p (c i) t -> p c t i", i=4),
+                        w_raw[:, :, rows].rearrange("p t (c i) -> p c t i", i=4),
+                    )
+
+        w_codes = keep.tile([P, N], U32, name="w_codes", align_bytes=64)
+        w_plane = keep.tile([P, N], U8, name="w_plane", align_bytes=64)
+        nc.vector.quantize_mx(
+            out=w_codes[:].bitcast(FP8X4), scales=w_plane[:], in_=w_bf[:].rearrange("p m t -> p (m t)")
+        )
+
+        out_view = out.rearrange("(mb p) j -> p mb j", p=P)
+        for c in range(CHUNKS):
+            cols = slice(c * CHUNK, (c + 1) * CHUNK)
+            if c % 2 == 0:
+                num_half = keep.tile([P, PACK, HALF], F32, name="num%d" % c)
+                for t in range(PACK):
+                    nc.vector.scalar_tensor_tensor(
+                        num_half[:, t, :],
+                        win[t][:, c * CHUNK : c * CHUNK + HALF],
+                        1.32,
+                        both[c // 2][:, t, :],
+                        ALU.mult,
+                        ALU.add,
+                    )
+            num = num_half[:, :, (c % 2) * CHUNK : (c % 2 + 1) * CHUNK]
+            z = keep.tile([P, CHUNK, PACK], BF16, name="z%d" % c, align_bytes=64)
+            nc.vector.tensor_tensor(
+                z[:].rearrange("p (c i) t -> p c t i", i=4),
+                num.rearrange("p t (c i) -> p c t i", i=4),
+                inv_root[c][:].rearrange("p t (c i) -> p c t i", i=4),
+                ALU.mult,
+            )
+            z_codes = keep.tile([P, CHUNK], U32, name="z_codes%d" % c, align_bytes=64)
+            z_plane = keep.tile([P, CHUNK], U8, name="z_plane%d" % c, align_bytes=64)
+            nc.vector.quantize_mx(
+                out=z_codes[:].bitcast(FP8X4), scales=z_plane[:], in_=z[:].rearrange("p j t -> p (j t)")
+            )
+            result = bank([P, N // P, CHUNK], "product%d" % c)
+            for mb in range(N // P):
+                rows = slice(mb * P, (mb + 1) * P)
+                nc.tensor.matmul_mx(
+                    out=result[:, mb, :],
+                    lhsT=w_codes[:, rows].bitcast(FP8X4),
+                    lhsT_scale=w_plane[:, rows],
+                    rhs=z_codes[:].bitcast(FP8X4),
+                    rhs_scale=z_plane[:],
+                    start=True,
+                    stop=True,
+                )
+            staged_out = keep.tile([P, N // P, CHUNK], F32, name="staged_out%d" % c)
+            nc.scalar.copy(staged_out[:], result[:])
+            nc.sync.dma_start(out=out_view[:, :, cols], in_=staged_out[:])

@@ -46,11 +46,11 @@ def tile_picked_scorestd_none_p_kernel(
         x_table = keep.tile([P, TABLE], U32, name="x_table")
         gn_sb = keep.tile([P, PACK], F32, name="gn_sb")
 
-        nc.vector.memset(d_bytes[:].bitcast(I32), 0)
+        nc.gpsimd.memset(d_bytes[:].bitcast(I32), 0)
         nc.vector.memset(x_bytes[:].bitcast(I32), 0)
         nc.sync.dma_start(kidx_sb[:], kidx)
-        nc.sync.dma_start(offs_sb[:], offs)
         nc.sync.dma_start(out=d_bytes[0:P:8, :].bitcast(I32), in_=d_scales[0].bitcast(I32))
+        nc.sync.dma_start(offs_sb[:], offs)
         nc.sync.dma_start(out=x_bytes[0:P:8, :].bitcast(I32), in_=x_scales[0].bitcast(I32))
         nc.sync.dma_start(n1_sb[:], n1)
         nc.sync.dma_start(n2_sb[:], n2)
@@ -64,7 +64,7 @@ def tile_picked_scorestd_none_p_kernel(
         nc.vector.memset(planes[:].bitcast(I32), 0)
 
         warm = keep.tile([P, 1], F32, name="warm")
-        nc.scalar.activation(warm[:], ident[:, 0:1], ACT.Abs_reciprocal_sqrt, bias=1.0)
+        nc.scalar.activation(warm[:], gn_sb[:, 0:1], ACT.Abs_reciprocal_sqrt, bias=1.0, scale=0.0)
 
         d_bytes_picked = keep.tile([P, H], U8, name="d_bytes_picked")
         x_bytes_picked = keep.tile([P, S], U8, name="x_bytes_picked")
@@ -72,8 +72,8 @@ def tile_picked_scorestd_none_p_kernel(
         nc.vector.tensor_copy(d_bytes_picked[:], d_bytes[:].indirect(kidx_sb[:]))
         nc.vector.tensor_copy(x_bytes_picked[:], x_bytes[:].indirect(offs_sb[:]))
         nc.vector.tensor_copy(
-            staged[:, 0:H].rearrange("p (t m) -> p m t", t=PACK),
-            d_bytes_picked[:].rearrange("p (m t) -> p m t", t=PACK),
+            staged[:, 0:H].rearrange("p (t g i) -> p g t i", t=PACK, i=16),
+            d_bytes_picked[:].rearrange("p (g i t) -> p g t i", t=PACK, i=16),
         )
         nc.vector.tensor_copy(staged[:, H : H + S].bitcast(I32), x_bytes_picked[:].bitcast(I32))
         for r in range(4):
@@ -83,23 +83,23 @@ def tile_picked_scorestd_none_p_kernel(
         d_dealt = keep.tile([P, H], U32, name="d_dealt", align_bytes=64)
         nc.vector.tensor_copy(d_picked[:], d_table[:].indirect(kidx_sb[:]))
         nc.vector.tensor_copy(
-            d_dealt[:].rearrange("p (t m) -> p m t", t=PACK),
-            d_picked[:].rearrange("p (m t) -> p m t", t=PACK),
+            d_dealt[:].rearrange("p (t g i) -> p g t i", t=PACK, i=4),
+            d_picked[:].rearrange("p (g i t) -> p g t i", t=PACK, i=4),
         )
         w_raw = keep.tile([P, PACK, N], F32, name="w_raw", tag="big_a")
         nc.sync.dma_start(out=w_raw[:], in_=w1.rearrange("(p t) m -> p t m", t=PACK))
 
-        row_scale = keep.tile([P, PACK], F32, name="row_scale")
+        row_scale = keep.tile([P, PACK], F32, name="row_scale", tag="later")
+        gn_sq = keep.tile([P, PACK], F32, name="gn_sq")
         gn_safe = keep.tile([P, PACK], F32, name="gn_safe")
-        gn_inv = keep.tile([P, PACK], F32, name="gn_inv")
         gn_inv_sq = keep.tile([P, PACK], F32, name="gn_inv_sq")
-        nc.vector.tensor_scalar(row_scale[:], gn_sb[:], 0.0625 * 0.3125 / 0.6, None, ALU.mult)
-        nc.vector.scalar_tensor_tensor(gn_safe[:], gn_sb[:], 0.0, gn_sb[:], ALU.is_equal, ALU.add)
-        nc.vector.reciprocal(gn_inv[:], gn_safe[:])
-        nc.vector.tensor_tensor(gn_inv_sq[:], gn_inv[:], gn_inv[:], ALU.mult)
+        nc.scalar.activation(row_scale[:], gn_sb[:], ACT.Copy, scale=0.0625 * 0.3125 / 0.6)
+        nc.scalar.activation(gn_sq[:], gn_sb[:], ACT.Square)
+        nc.scalar.activation(gn_safe[:], gn_sq[:], ACT.Identity, bias=1e-37)
+        nc.vector.reciprocal(gn_inv_sq[:], gn_safe[:])
 
         x_picked = keep.tile([P, S], U32, name="x_picked", align_bytes=64)
-        scores = [bank([P, S], "product%d" % t) for t in range(PACK)]
+        scores = [bank([P, 2, HALF], "product%d" % t) for t in range(PACK)]
         win = [keep.tile([P, S], F32, name="win%d" % t) for t in range(PACK)]
         for h in range(2):
             cols = slice(h * HALF, (h + 1) * HALF)
@@ -109,7 +109,7 @@ def tile_picked_scorestd_none_p_kernel(
             for h in range(2):
                 cols = slice(h * HALF, (h + 1) * HALF)
                 nc.tensor.matmul_mx(
-                    out=scores[t][:, cols],
+                    out=scores[2 * (t // 2) + h][:, t % 2, :],
                     lhsT=d_dealt[:, keys].bitcast(FP8X4),
                     lhsT_scale=planes[:, keys],
                     rhs=x_picked[:, cols].bitcast(FP8X4),
@@ -117,7 +117,9 @@ def tile_picked_scorestd_none_p_kernel(
                     start=True,
                     stop=True,
                 )
-            nc.scalar.activation(win[t][:], scores[t][:], ACT.Copy, scale=row_scale[:, t : t + 1])
+                nc.scalar.activation(
+                    win[t][:, cols], scores[2 * (t // 2) + h][:, t % 2, :], ACT.Copy, scale=row_scale[:, t : t + 1]
+                )
 
         def add_turned(dst, first, second):
             nc.tensor.matmul(dst, first, ident[:], start=True, stop=False, is_transpose=True)
@@ -125,16 +127,19 @@ def tile_picked_scorestd_none_p_kernel(
 
         both = [keep.tile([P, PACK, HALF], F32, name="both%d" % h) for h in range(2)]
         inv_root = []
+        first = keep.tile([P, 2, PACK, CHUNK], F32, name="first")
+        later = keep.tile([P, CHUNKS - 1, 2, PACK, CHUNK], F32, name="later", tag="later")
         for c in range(CHUNKS):
             cols = slice(c * CHUNK, (c + 1) * CHUNK)
             entries = slice(c * CHUNK // 16, (c + 1) * CHUNK // 16)
-            a_neg = keep.tile([P, PACK, CHUNK], F32, name="a_neg%d" % c)
-            b_pos = keep.tile([P, PACK, CHUNK], F32, name="b_pos%d" % c)
+            fetched = first[:] if c == 0 else later[:, c - 1]
+            a_neg = fetched[:, 0]
+            b_pos = fetched[:, 1]
             for t in range(PACK):
                 nc.vector.tensor_scalar(a_neg[:, t, :], win[t][:].indirect(n1_sb[:, entries]), -0.6, 0.0, ALU.mult, ALU.add)
                 nc.vector.tensor_scalar(b_pos[:, t, :], win[t][:].indirect(n2_sb[:, entries]), 0.6, 0.0, ALU.mult, ALU.add)
             u = both[c // 2][:, :, (c % 2) * CHUNK : (c % 2 + 1) * CHUNK]
-            nc.vector.tensor_tensor(u, a_neg[:], b_pos[:], ALU.subtract)
+            nc.vector.tensor_tensor(u, a_neg, b_pos, ALU.subtract)
 
             diff_t = bank([P, PACK, P], "turned%d" % min(c, 1))
             for t in range(PACK):

@@ -42,8 +42,8 @@ def tile_picked_scorestd_none_p_kernel(
         n2_sb = keep.tile([P, S // 16], U16, name="n2_sb")
         d_bytes = keep.tile([P, TABLE], U8, name="d_bytes")
         x_bytes = keep.tile([P, TABLE], U8, name="x_bytes")
-        d_table = keep.tile([P, TABLE], U32, name="d_table", tag="big_a")
-        x_table = keep.tile([P, TABLE], U32, name="x_table")
+        d_table = keep.tile([P, TABLE], U32, name="d_table")
+        x_table = keep.tile([P, TABLE], U32, name="x_table", tag="big_a")
         gn_sb = keep.tile([P, PACK], F32, name="gn_sb")
 
         nc.gpsimd.memset(d_bytes[:].bitcast(I32), 0)
@@ -52,11 +52,11 @@ def tile_picked_scorestd_none_p_kernel(
         nc.sync.dma_start(out=d_bytes[0:P:8, :].bitcast(I32), in_=d_scales[0].bitcast(I32))
         nc.sync.dma_start(offs_sb[:], offs)
         nc.sync.dma_start(out=x_bytes[0:P:8, :].bitcast(I32), in_=x_scales[0].bitcast(I32))
-        nc.sync.dma_start(n1_sb[:], n1)
-        nc.sync.dma_start(n2_sb[:], n2)
         nc.scalar.dma_start(out=gn_sb[:], in_=gn.rearrange("(p t) o -> p (t o)", t=PACK))
         nc.sync.dma_start(out=d_table[:].bitcast(I32), in_=d_words[0].rearrange("p n t -> p (n t)").bitcast(I32))
         nc.sync.dma_start(out=x_table[:].bitcast(I32), in_=x_words[0].rearrange("p n t -> p (n t)").bitcast(I32))
+        nc.sync.dma_start(n1_sb[:], n1)
+        nc.sync.dma_start(n2_sb[:], n2)
 
         ident = keep.tile([P, P], F32, name="ident")
         make_identity(nc, ident[:])
@@ -86,8 +86,6 @@ def tile_picked_scorestd_none_p_kernel(
             d_dealt[:].rearrange("p (t g i) -> p g t i", t=PACK, i=4),
             d_picked[:].rearrange("p (g i t) -> p g t i", t=PACK, i=4),
         )
-        w_raw = keep.tile([P, PACK, N], F32, name="w_raw", tag="big_a")
-        nc.sync.dma_start(out=w_raw[:], in_=w1.rearrange("(p t) m -> p t m", t=PACK))
 
         row_scale = keep.tile([P, PACK], F32, name="row_scale", tag="later")
         gn_sq = keep.tile([P, PACK], F32, name="gn_sq")
@@ -104,6 +102,8 @@ def tile_picked_scorestd_none_p_kernel(
         for h in range(2):
             cols = slice(h * HALF, (h + 1) * HALF)
             nc.vector.tensor_copy(x_picked[:, cols], x_table[:].indirect(offs_sb[:, h * 16 : (h + 1) * 16]))
+        w_raw = keep.tile([P, PACK, N], F32, name="w_raw", tag="big_a")
+        nc.sync.dma_start(out=w_raw[:], in_=w1.rearrange("(p t) m -> p t m", t=PACK))
         for t in range(PACK):
             keys = slice(t * P, (t + 1) * P)
             for h in range(2):
@@ -126,42 +126,69 @@ def tile_picked_scorestd_none_p_kernel(
             nc.tensor.matmul(dst, second, ident[:], start=False, stop=True, is_transpose=True)
 
         both = [keep.tile([P, PACK, HALF], F32, name="both%d" % h) for h in range(2)]
-        inv_root = []
-        first = keep.tile([P, 2, PACK, CHUNK], F32, name="first")
-        later = keep.tile([P, CHUNKS - 1, 2, PACK, CHUNK], F32, name="later", tag="later")
-        for c in range(CHUNKS):
-            cols = slice(c * CHUNK, (c + 1) * CHUNK)
-            entries = slice(c * CHUNK // 16, (c + 1) * CHUNK // 16)
-            fetched = first[:] if c == 0 else later[:, c - 1]
+        inv_root = [keep.tile([P, PACK, HALF], F32, name="inv_root%d" % h) for h in range(2)]
+        first = keep.tile([P, 2, PACK, HALF], F32, name="first")
+        later = keep.tile([P, 2, PACK, HALF], F32, name="later", tag="later")
+        for step in range(4):
+            h, pair = divmod(step, 2)
+            tiles = (2 * pair, 2 * pair + 1)
+            pair_rows = slice(2 * pair, 2 * pair + 2)
+            entries = slice(h * HALF // 16, (h + 1) * HALF // 16)
+            fetched = first if h == 0 else later
             a_neg = fetched[:, 0]
             b_pos = fetched[:, 1]
-            for t in range(PACK):
+            for t in tiles:
                 nc.vector.tensor_scalar(a_neg[:, t, :], win[t][:].indirect(n1_sb[:, entries]), -0.6, 0.0, ALU.mult, ALU.add)
                 nc.vector.tensor_scalar(b_pos[:, t, :], win[t][:].indirect(n2_sb[:, entries]), 0.6, 0.0, ALU.mult, ALU.add)
-            u = both[c // 2][:, :, (c % 2) * CHUNK : (c % 2 + 1) * CHUNK]
-            nc.vector.tensor_tensor(u, a_neg, b_pos, ALU.subtract)
+            nc.vector.tensor_tensor(both[h][:, pair_rows, :], a_neg[:, pair_rows, :], b_pos[:, pair_rows, :], ALU.subtract)
 
-            diff_t = bank([P, PACK, P], "turned%d" % min(c, 1))
-            for t in range(PACK):
-                add_turned(diff_t[:, t, :], a_neg[:, t, :], b_pos[:, t, :])
-            diff_sq = keep.tile([P, PACK, P], F32, name="diff_sq%d" % c)
+            if step == 3:
+                half = slice(h * HALF, (h + 1) * HALF)
+                diff = keep.tile([P, 2, HALF], F32, name="diff")
+                nc.vector.tensor_tensor(diff[:], a_neg[:, pair_rows, :], b_pos[:, pair_rows, :], ALU.add)
+                mean = keep.tile([P, 2, HALF], F32, name="mean")
+                for n, t in enumerate(tiles):
+                    nc.vector.tensor_tensor(mean[:, n, :], win[t][:, half], both[h][:, t, :], ALU.add)
+                diff_sq = keep.tile([P, 2, HALF], F32, name="diff_sq3")
+                mean_sq = keep.tile([P, 2, HALF], F32, name="mean_sq3")
+                nc.scalar.activation(diff_sq[:], diff[:], ACT.Square, scale=1.6)
+                nc.scalar.activation(mean_sq[:], mean[:], ACT.Square, scale=0.6)
+                total = keep.tile([P, 2, HALF], F32, name="total")
+                nc.vector.tensor_tensor(total[:], diff_sq[:], mean_sq[:], ALU.add)
+                for n, t in enumerate(tiles):
+                    nc.scalar.activation(
+                        inv_root[h][:, t, :],
+                        total[:, n, :],
+                        ACT.Abs_reciprocal_sqrt,
+                        bias=0.1,
+                        scale=gn_inv_sq[:, t : t + 1],
+                    )
+                continue
+
+            blocks = [(t, slice(k * P, (k + 1) * P)) for t in tiles for k in range(HALF // P)]
+            diff_t = bank([P, 4, P], "turned%d" % min(step, 1))
+            for n, (t, cols) in enumerate(blocks):
+                add_turned(diff_t[:, n, :], a_neg[:, t, cols], b_pos[:, t, cols])
+            diff_sq = keep.tile([P, 4, P], F32, name="diff_sq%d" % step)
             nc.scalar.activation(diff_sq[:], diff_t[:], ACT.Square, scale=1.6)
-            mean_t = bank([P, PACK, P], "turned%d" % (1 - min(c, 1)))
-            for t in range(PACK):
-                add_turned(mean_t[:, t, :], win[t][:, cols], u[:, t, :])
-            mean_sq = keep.tile([P, PACK, P], F32, name="mean_sq%d" % c)
+            mean_t = bank([P, 4, P], "turned%d" % (1 - min(step, 1)))
+            for n, (t, cols) in enumerate(blocks):
+                add_turned(mean_t[:, n, :], win[t][:, h * HALF : (h + 1) * HALF][:, cols], both[h][:, t, cols])
+            mean_sq = keep.tile([P, 4, P], F32, name="mean_sq%d" % step)
             nc.scalar.activation(mean_sq[:], mean_t[:], ACT.Square, scale=0.6)
-            spread = bank([P, PACK, CHUNK], "spread%d" % (c % 2))
-            for t in range(PACK):
-                add_turned(spread[:, t, :], diff_sq[:, t, :], mean_sq[:, t, :])
-            r = keep.tile([P, PACK, CHUNK], F32, name="inv_root%d" % c)
-            for t in range(PACK):
+            spread = bank([P, 4, P], "spread%d" % (step % 2))
+            for n in range(4):
+                add_turned(spread[:, n, :], diff_sq[:, n, :], mean_sq[:, n, :])
+            for n, t in enumerate(tiles):
                 nc.scalar.activation(
-                    r[:, t, :], spread[:, t, :], ACT.Abs_reciprocal_sqrt, bias=0.1, scale=gn_inv_sq[:, t : t + 1]
+                    inv_root[h][:, t, :],
+                    spread[:, 2 * n : 2 * n + 2, :].rearrange("p k j -> p (k j)"),
+                    ACT.Abs_reciprocal_sqrt,
+                    bias=0.1,
+                    scale=gn_inv_sq[:, t : t + 1],
                 )
-            inv_root.append(r)
 
-            if c == 0:
+            if step == 0:
                 w_bf = keep.tile([P, N, PACK], BF16, name="w_bf", align_bytes=64)
                 for mb in range(N // P):
                     rows = slice(mb * P, (mb + 1) * P)
@@ -177,44 +204,44 @@ def tile_picked_scorestd_none_p_kernel(
         )
 
         out_view = out.rearrange("(mb p) j -> p mb j", p=P)
-        for c in range(CHUNKS):
-            cols = slice(c * CHUNK, (c + 1) * CHUNK)
-            if c % 2 == 0:
-                num_half = keep.tile([P, PACK, HALF], F32, name="num%d" % c)
+        result_banks = ["product0", "product1", "product2", "product3", "spread0", "turned0"]
+        for piece, (start, width) in enumerate(((0, 256), (256, 128), (384, 128))):
+            h, inside = divmod(start, HALF)
+            if inside == 0:
+                num = keep.tile([P, PACK, HALF], F32, name="num", tag="num")
                 for t in range(PACK):
                     nc.vector.scalar_tensor_tensor(
-                        num_half[:, t, :],
-                        win[t][:, c * CHUNK : c * CHUNK + HALF],
-                        1.32,
-                        both[c // 2][:, t, :],
-                        ALU.mult,
-                        ALU.add,
+                        num[:, t, :], win[t][:, start : start + HALF], 1.32, both[h][:, t, :], ALU.mult, ALU.add
                     )
-            num = num_half[:, :, (c % 2) * CHUNK : (c % 2 + 1) * CHUNK]
-            z = keep.tile([P, CHUNK, PACK], BF16, name="z%d" % c, align_bytes=64)
+            part = slice(inside, inside + width)
+            z = keep.tile([P, width, PACK], BF16, name="z%d" % piece, align_bytes=64)
             nc.vector.tensor_tensor(
                 z[:].rearrange("p (c i) t -> p c t i", i=4),
-                num.rearrange("p t (c i) -> p c t i", i=4),
-                inv_root[c][:].rearrange("p t (c i) -> p c t i", i=4),
+                num[:, :, part].rearrange("p t (c i) -> p c t i", i=4),
+                inv_root[h][:, :, part].rearrange("p t (c i) -> p c t i", i=4),
                 ALU.mult,
             )
-            z_codes = keep.tile([P, CHUNK], U32, name="z_codes%d" % c, align_bytes=64)
-            z_plane = keep.tile([P, CHUNK], U8, name="z_plane%d" % c, align_bytes=64)
+            z_codes = keep.tile([P, width], U32, name="z_codes%d" % piece, align_bytes=64)
+            z_plane = keep.tile([P, width], U8, name="z_plane%d" % piece, align_bytes=64)
             nc.vector.quantize_mx(
                 out=z_codes[:].bitcast(FP8X4), scales=z_plane[:], in_=z[:].rearrange("p j t -> p (j t)")
             )
-            result = bank([P, N // P, CHUNK], "product%d" % c)
-            for mb in range(N // P):
-                rows = slice(mb * P, (mb + 1) * P)
-                nc.tensor.matmul_mx(
-                    out=result[:, mb, :],
-                    lhsT=w_codes[:, rows].bitcast(FP8X4),
-                    lhsT_scale=w_plane[:, rows],
-                    rhs=z_codes[:].bitcast(FP8X4),
-                    rhs_scale=z_plane[:],
-                    start=True,
-                    stop=True,
-                )
-            staged_out = keep.tile([P, N // P, CHUNK], F32, name="staged_out%d" % c)
-            nc.scalar.copy(staged_out[:], result[:])
-            nc.sync.dma_start(out=out_view[:, :, cols], in_=staged_out[:])
+            for side in range(2):
+                result = bank([P, 2, width], result_banks[2 * piece + side])
+                for n in range(2):
+                    rows = slice((2 * side + n) * P, (2 * side + n + 1) * P)
+                    nc.tensor.matmul_mx(
+                        out=result[:, n, :],
+                        lhsT=w_codes[:, rows].bitcast(FP8X4),
+                        lhsT_scale=w_plane[:, rows],
+                        rhs=z_codes[:].bitcast(FP8X4),
+                        rhs_scale=z_plane[:],
+                        start=True,
+                        stop=True,
+                    )
+                staged_out = keep.tile([P, 2, width], F32, name="staged_out%d_%d" % (piece, side))
+                if piece == 2 and side == 1:
+                    nc.vector.tensor_copy(staged_out[:], result[:])
+                else:
+                    nc.scalar.copy(staged_out[:], result[:])
+                nc.sync.dma_start(out=out_view[:, 2 * side : 2 * side + 2, start : start + width], in_=staged_out[:])

@@ -58,8 +58,6 @@ def tile_picked_scorestd_none_p_kernel(
         nc.sync.dma_start(n1_sb[:], n1)
         nc.sync.dma_start(n2_sb[:], n2)
 
-        ident = keep.tile([P, P], F32, name="ident")
-        make_identity(nc, ident[:])
         planes = keep.tile([P, H + S], U8, name="planes", align_bytes=64)
         nc.vector.memset(planes[:].bitcast(I32), 0)
 
@@ -89,12 +87,9 @@ def tile_picked_scorestd_none_p_kernel(
 
         row_scale = keep.tile([P, PACK], F32, name="row_scale", tag="later")
         gn_sq = keep.tile([P, PACK], F32, name="gn_sq")
-        gn_safe = keep.tile([P, PACK], F32, name="gn_safe")
         gn_inv_sq = keep.tile([P, PACK], F32, name="gn_inv_sq")
         nc.scalar.activation(row_scale[:], gn_sb[:], ACT.Copy, scale=0.0625 * 0.3125 / 0.6)
         nc.scalar.activation(gn_sq[:], gn_sb[:], ACT.Square)
-        nc.scalar.activation(gn_safe[:], gn_sq[:], ACT.Identity, bias=1e-37)
-        nc.vector.reciprocal(gn_inv_sq[:], gn_safe[:])
 
         x_picked = keep.tile([P, S], U32, name="x_picked", align_bytes=64)
         scores = [bank([P, 2, HALF], "product%d" % t) for t in range(PACK)]
@@ -102,6 +97,9 @@ def tile_picked_scorestd_none_p_kernel(
         for h in range(2):
             cols = slice(h * HALF, (h + 1) * HALF)
             nc.vector.tensor_copy(x_picked[:, cols], x_table[:].indirect(offs_sb[:, h * 16 : (h + 1) * 16]))
+        gn_safe = keep.tile([P, PACK], F32, name="gn_safe", tag="big_a")
+        nc.scalar.activation(gn_safe[:], gn_sq[:], ACT.Identity, bias=1e-37)
+        nc.vector.reciprocal(gn_inv_sq[:], gn_safe[:])
         w_raw = keep.tile([P, PACK, N], F32, name="w_raw", tag="big_a")
         nc.sync.dma_start(out=w_raw[:], in_=w1.rearrange("(p t) m -> p t m", t=PACK))
         for t in range(PACK):
@@ -120,6 +118,9 @@ def tile_picked_scorestd_none_p_kernel(
                 nc.scalar.activation(
                     win[t][:, cols], scores[2 * (t // 2) + h][:, t % 2, :], ACT.Copy, scale=row_scale[:, t : t + 1]
                 )
+
+        ident = keep.tile([P, P], F32, name="ident")
+        make_identity(nc, ident[:])
 
         def add_turned(dst, first, second):
             nc.tensor.matmul(dst, first, ident[:], start=True, stop=False, is_transpose=True)
@@ -140,7 +141,8 @@ def tile_picked_scorestd_none_p_kernel(
             for t in tiles:
                 nc.vector.tensor_scalar(a_neg[:, t, :], win[t][:].indirect(n1_sb[:, entries]), -0.6, 0.0, ALU.mult, ALU.add)
                 nc.vector.tensor_scalar(b_pos[:, t, :], win[t][:].indirect(n2_sb[:, entries]), 0.6, 0.0, ALU.mult, ALU.add)
-            nc.vector.tensor_tensor(both[h][:, pair_rows, :], a_neg[:, pair_rows, :], b_pos[:, pair_rows, :], ALU.subtract)
+            adder = nc.vector if step == 3 else nc.gpsimd
+            adder.tensor_tensor(both[h][:, pair_rows, :], a_neg[:, pair_rows, :], b_pos[:, pair_rows, :], ALU.subtract)
 
             if step == 3:
                 half = slice(h * HALF, (h + 1) * HALF)
@@ -149,8 +151,8 @@ def tile_picked_scorestd_none_p_kernel(
                 mean = keep.tile([P, 2, HALF], F32, name="mean")
                 for n, t in enumerate(tiles):
                     nc.vector.tensor_tensor(mean[:, n, :], win[t][:, half], both[h][:, t, :], ALU.add)
-                diff_sq = keep.tile([P, 2, HALF], F32, name="diff_sq3")
-                mean_sq = keep.tile([P, 2, HALF], F32, name="mean_sq3")
+                diff_sq = keep.tile([P, 2, HALF], F32, name="diff_sq3", tag="diff_sq1")
+                mean_sq = keep.tile([P, 2, HALF], F32, name="mean_sq3", tag="mean_sq1", align_bytes=64)
                 nc.scalar.activation(diff_sq[:], diff[:], ACT.Square, scale=1.6)
                 nc.scalar.activation(mean_sq[:], mean[:], ACT.Square, scale=0.6)
                 total = keep.tile([P, 2, HALF], F32, name="total")
@@ -169,12 +171,12 @@ def tile_picked_scorestd_none_p_kernel(
             diff_t = bank([P, 4, P], "turned%d" % min(step, 1))
             for n, (t, cols) in enumerate(blocks):
                 add_turned(diff_t[:, n, :], a_neg[:, t, cols], b_pos[:, t, cols])
-            diff_sq = keep.tile([P, 4, P], F32, name="diff_sq%d" % step)
+            diff_sq = keep.tile([P, 4, P], F32, name="diff_sq%d" % step, tag="diff_sq%d" % step)
             nc.scalar.activation(diff_sq[:], diff_t[:], ACT.Square, scale=1.6)
             mean_t = bank([P, 4, P], "turned%d" % (1 - min(step, 1)))
             for n, (t, cols) in enumerate(blocks):
                 add_turned(mean_t[:, n, :], win[t][:, h * HALF : (h + 1) * HALF][:, cols], both[h][:, t, cols])
-            mean_sq = keep.tile([P, 4, P], F32, name="mean_sq%d" % step)
+            mean_sq = keep.tile([P, 4, P], F32, name="mean_sq%d" % step, tag="mean_sq%d" % step, align_bytes=64)
             nc.scalar.activation(mean_sq[:], mean_t[:], ACT.Square, scale=0.6)
             spread = bank([P, 4, P], "spread%d" % (step % 2))
             for n in range(4):
@@ -214,7 +216,8 @@ def tile_picked_scorestd_none_p_kernel(
                         num[:, t, :], win[t][:, start : start + HALF], 1.32, both[h][:, t, :], ALU.mult, ALU.add
                     )
             part = slice(inside, inside + width)
-            z = keep.tile([P, width, PACK], BF16, name="z%d" % piece, align_bytes=64)
+            z_tag = "mean_sq1" if piece == 0 else "z%d" % piece
+            z = keep.tile([P, width, PACK], BF16, name="z%d" % piece, tag=z_tag, align_bytes=64)
             nc.vector.tensor_tensor(
                 z[:].rearrange("p (c i) t -> p c t i", i=4),
                 num[:, :, part].rearrange("p t (c i) -> p c t i", i=4),

@@ -15,14 +15,28 @@ ACT = mybir.ActivationFunctionType
 
 P = 128
 PACK = 4
+K = 512
 TABLE = 2048
-S = 512
 H = 512
+S = 512
 N = 512
-CHUNK = 128
-CHUNKS = S // CHUNK
 HALF = S // 2
-FLOPS = 2 * 512 * H * S + 2 * H * N * S
+LIST_ROWS = 16
+QUADRANT = 32
+BLOCK_ROWS = 8
+FLOPS = 2 * K * H * S + 2 * H * N * S
+
+SCORE = 0.0625
+MEAN = 0.3125
+EPS = 0.1
+FETCH = (1 - 2 * MEAN) / (2 * MEAN)
+NUM_W = (1 - MEAN) * FETCH / MEAN
+DIFF_SCALE = 0.5 / MEAN
+TINY = 1e-30
+
+STEPS = 4
+LAST_STEP = STEPS - 1
+PIECES = ((0, 256), (256, 128), (384, 128))
 
 
 def tile_picked_scorestd_none_p_kernel(
@@ -36,22 +50,22 @@ def tile_picked_scorestd_none_p_kernel(
         def bank(shape, tag):
             return psum.tile(shape, F32, name=tag, tag=tag)
 
-        kidx_sb = keep.tile([P, H // 16], U16, name="kidx_sb")
-        offs_sb = keep.tile([P, S // 16], U16, name="offs_sb")
-        n1_sb = keep.tile([P, S // 16], U16, name="n1_sb")
-        n2_sb = keep.tile([P, S // 16], U16, name="n2_sb")
+        kidx_sb = keep.tile([P, H // LIST_ROWS], U16, name="kidx_sb")
+        offs_sb = keep.tile([P, S // LIST_ROWS], U16, name="offs_sb")
+        n1_sb = keep.tile([P, S // LIST_ROWS], U16, name="n1_sb")
+        n2_sb = keep.tile([P, S // LIST_ROWS], U16, name="n2_sb")
         d_bytes = keep.tile([P, TABLE], U8, name="d_bytes")
         x_bytes = keep.tile([P, TABLE], U8, name="x_bytes")
         d_table = keep.tile([P, TABLE], U32, name="d_table")
-        x_table = keep.tile([P, TABLE], U32, name="x_table", tag="big_a")
+        x_table = keep.tile([P, TABLE], U32, name="x_table", tag="after_x")
         gn_sb = keep.tile([P, PACK], F32, name="gn_sb")
 
         nc.gpsimd.memset(d_bytes[:].bitcast(I32), 0)
         nc.vector.memset(x_bytes[:].bitcast(I32), 0)
         nc.sync.dma_start(kidx_sb[:], kidx)
-        nc.sync.dma_start(out=d_bytes[0:P:8, :].bitcast(I32), in_=d_scales[0].bitcast(I32))
+        nc.sync.dma_start(out=d_bytes[0:P:BLOCK_ROWS, :].bitcast(I32), in_=d_scales[0].bitcast(I32))
         nc.sync.dma_start(offs_sb[:], offs)
-        nc.sync.dma_start(out=x_bytes[0:P:8, :].bitcast(I32), in_=x_scales[0].bitcast(I32))
+        nc.sync.dma_start(out=x_bytes[0:P:BLOCK_ROWS, :].bitcast(I32), in_=x_scales[0].bitcast(I32))
         nc.scalar.dma_start(out=gn_sb[:], in_=gn.rearrange("(p t) o -> p (t o)", t=PACK))
         nc.sync.dma_start(out=d_table[:].bitcast(I32), in_=d_words[0].rearrange("p n t -> p (n t)").bitcast(I32))
         nc.sync.dma_start(out=x_table[:].bitcast(I32), in_=x_words[0].rearrange("p n t -> p (n t)").bitcast(I32))
@@ -60,10 +74,6 @@ def tile_picked_scorestd_none_p_kernel(
 
         planes = keep.tile([P, H + S], U8, name="planes", align_bytes=64)
         nc.vector.memset(planes[:].bitcast(I32), 0)
-
-        warm = keep.tile([P, 1], F32, name="warm")
-        nc.scalar.activation(warm[:], gn_sb[:, 0:1], ACT.Abs_reciprocal_sqrt, bias=1.0, scale=0.0)
-
         d_bytes_picked = keep.tile([P, H], U8, name="d_bytes_picked")
         x_bytes_picked = keep.tile([P, S], U8, name="x_bytes_picked")
         staged = keep.tile([P, H + S], U8, name="staged")
@@ -74,8 +84,10 @@ def tile_picked_scorestd_none_p_kernel(
             d_bytes_picked[:].rearrange("p (g i t) -> p g t i", t=PACK, i=16),
         )
         nc.vector.tensor_copy(staged[:, H : H + S].bitcast(I32), x_bytes_picked[:].bitcast(I32))
-        for r in range(4):
-            nc.scalar.dma_start(out=planes[r:P:32, :].bitcast(I32), in_=staged[8 * r : P : 32, :].bitcast(I32))
+        for r in range(QUADRANT // BLOCK_ROWS):
+            nc.scalar.dma_start(
+                out=planes[r:P:QUADRANT, :].bitcast(I32), in_=staged[BLOCK_ROWS * r : P : QUADRANT, :].bitcast(I32)
+            )
 
         d_picked = keep.tile([P, H], U32, name="d_picked")
         d_dealt = keep.tile([P, H], U32, name="d_dealt", align_bytes=64)
@@ -85,39 +97,39 @@ def tile_picked_scorestd_none_p_kernel(
             d_picked[:].rearrange("p (g i t) -> p g t i", t=PACK, i=4),
         )
 
-        row_scale = keep.tile([P, PACK], F32, name="row_scale", tag="later")
+        row_scale = keep.tile([P, PACK], F32, name="row_scale", tag="after_windows")
         gn_sq = keep.tile([P, PACK], F32, name="gn_sq")
+        gn_inv = keep.tile([P, PACK], F32, name="gn_inv")
         gn_inv_sq = keep.tile([P, PACK], F32, name="gn_inv_sq")
-        nc.scalar.activation(row_scale[:], gn_sb[:], ACT.Copy, scale=0.0625 * 0.3125 / 0.6)
+        nc.scalar.activation(row_scale[:], gn_sb[:], ACT.Copy, scale=SCORE * MEAN / FETCH)
         nc.scalar.activation(gn_sq[:], gn_sb[:], ACT.Square)
+        nc.scalar.activation(gn_inv[:], gn_sq[:], ACT.Abs_reciprocal_sqrt, bias=TINY)
+        nc.scalar.activation(gn_inv_sq[:], gn_inv[:], ACT.Square)
 
         x_picked = keep.tile([P, S], U32, name="x_picked", align_bytes=64)
-        scores = [bank([P, 2, HALF], "product%d" % t) for t in range(PACK)]
         win = [keep.tile([P, S], F32, name="win%d" % t) for t in range(PACK)]
+        halves = [slice(h * HALF, (h + 1) * HALF) for h in range(2)]
+        entries = [slice(h * HALF // LIST_ROWS, (h + 1) * HALF // LIST_ROWS) for h in range(2)]
         for h in range(2):
-            cols = slice(h * HALF, (h + 1) * HALF)
-            nc.vector.tensor_copy(x_picked[:, cols], x_table[:].indirect(offs_sb[:, h * 16 : (h + 1) * 16]))
-        gn_safe = keep.tile([P, PACK], F32, name="gn_safe", tag="big_a")
-        nc.scalar.activation(gn_safe[:], gn_sq[:], ACT.Identity, bias=1e-37)
-        nc.vector.reciprocal(gn_inv_sq[:], gn_safe[:])
-        w_raw = keep.tile([P, PACK, N], F32, name="w_raw", tag="big_a")
+            nc.vector.tensor_copy(x_picked[:, halves[h]], x_table[:].indirect(offs_sb[:, entries[h]]))
+
+        w_raw = keep.tile([P, PACK, N], F32, name="w_raw", tag="after_x")
         nc.sync.dma_start(out=w_raw[:], in_=w1.rearrange("(p t) m -> p t m", t=PACK))
+
         for t in range(PACK):
             keys = slice(t * P, (t + 1) * P)
-            for h in range(2):
-                cols = slice(h * HALF, (h + 1) * HALF)
+            for n, cols in enumerate(halves if t < 2 else [slice(0, S)]):
+                scores = bank([P, cols.stop - cols.start], ("product%d" if n == 0 else "turned%d") % t)
                 nc.tensor.matmul_mx(
-                    out=scores[2 * (t // 2) + h][:, t % 2, :],
+                    out=scores[:],
                     lhsT=d_dealt[:, keys].bitcast(FP8X4),
                     lhsT_scale=planes[:, keys],
                     rhs=x_picked[:, cols].bitcast(FP8X4),
-                    rhs_scale=planes[:, H + h * HALF : H + (h + 1) * HALF],
+                    rhs_scale=planes[:, H + cols.start : H + cols.stop],
                     start=True,
                     stop=True,
                 )
-                nc.scalar.activation(
-                    win[t][:, cols], scores[2 * (t // 2) + h][:, t % 2, :], ACT.Copy, scale=row_scale[:, t : t + 1]
-                )
+                nc.scalar.activation(win[t][:, cols], scores[:], ACT.Copy, scale=row_scale[:, t : t + 1])
 
         ident = keep.tile([P, P], F32, name="ident")
         make_identity(nc, ident[:])
@@ -126,69 +138,59 @@ def tile_picked_scorestd_none_p_kernel(
             nc.tensor.matmul(dst, first, ident[:], start=True, stop=False, is_transpose=True)
             nc.tensor.matmul(dst, second, ident[:], start=False, stop=True, is_transpose=True)
 
+        def inverse_root(h, t, total):
+            nc.scalar.activation(
+                inv_root[h][:, t, :], total, ACT.Abs_reciprocal_sqrt, bias=EPS, scale=gn_inv_sq[:, t : t + 1]
+            )
+
         both = [keep.tile([P, PACK, HALF], F32, name="both%d" % h) for h in range(2)]
         inv_root = [keep.tile([P, PACK, HALF], F32, name="inv_root%d" % h) for h in range(2)]
-        first = keep.tile([P, 2, PACK, HALF], F32, name="first")
-        later = keep.tile([P, 2, PACK, HALF], F32, name="later", tag="later")
-        for step in range(4):
+        fetched_tags = ["fetched0", "fetched1", "after_windows", "fetched0"]
+        for step in range(STEPS):
             h, pair = divmod(step, 2)
             tiles = (2 * pair, 2 * pair + 1)
-            pair_rows = slice(2 * pair, 2 * pair + 2)
-            entries = slice(h * HALF // 16, (h + 1) * HALF // 16)
-            fetched = first if h == 0 else later
+            fetched = keep.tile([P, 2, 2, HALF], F32, name="fetched%d" % step, tag=fetched_tags[step])
             a_neg = fetched[:, 0]
             b_pos = fetched[:, 1]
-            for t in tiles:
-                nc.vector.tensor_scalar(a_neg[:, t, :], win[t][:].indirect(n1_sb[:, entries]), -0.6, 0.0, ALU.mult, ALU.add)
-                nc.vector.tensor_scalar(b_pos[:, t, :], win[t][:].indirect(n2_sb[:, entries]), 0.6, 0.0, ALU.mult, ALU.add)
-            adder = nc.vector if step == 3 else nc.gpsimd
-            adder.tensor_tensor(both[h][:, pair_rows, :], a_neg[:, pair_rows, :], b_pos[:, pair_rows, :], ALU.subtract)
+            for n, t in enumerate(tiles):
+                from_n1 = win[t][:].indirect(n1_sb[:, entries[h]])
+                from_n2 = win[t][:].indirect(n2_sb[:, entries[h]])
+                nc.vector.tensor_scalar(a_neg[:, n, :], from_n1, -FETCH, 0.0, ALU.mult, ALU.add)
+                nc.vector.tensor_scalar(b_pos[:, n, :], from_n2, FETCH, 0.0, ALU.mult, ALU.add)
+            adder = nc.vector if step == LAST_STEP else nc.gpsimd
+            adder.tensor_tensor(both[h][:, 2 * pair : 2 * pair + 2, :], a_neg, b_pos, ALU.subtract)
 
-            if step == 3:
-                half = slice(h * HALF, (h + 1) * HALF)
+            if step == LAST_STEP:
                 diff = keep.tile([P, 2, HALF], F32, name="diff")
-                nc.vector.tensor_tensor(diff[:], a_neg[:, pair_rows, :], b_pos[:, pair_rows, :], ALU.add)
+                nc.vector.tensor_tensor(diff[:], a_neg, b_pos, ALU.add)
                 mean = keep.tile([P, 2, HALF], F32, name="mean")
                 for n, t in enumerate(tiles):
-                    nc.vector.tensor_tensor(mean[:, n, :], win[t][:, half], both[h][:, t, :], ALU.add)
-                diff_sq = keep.tile([P, 2, HALF], F32, name="diff_sq3", tag="diff_sq1")
-                mean_sq = keep.tile([P, 2, HALF], F32, name="mean_sq3", tag="mean_sq1", align_bytes=64)
-                nc.scalar.activation(diff_sq[:], diff[:], ACT.Square, scale=1.6)
-                nc.scalar.activation(mean_sq[:], mean[:], ACT.Square, scale=0.6)
+                    nc.vector.tensor_tensor(mean[:, n, :], win[t][:, halves[h]], both[h][:, t, :], ALU.add)
+                squares = keep.tile([P, 2, 2, HALF], F32, name="squares", tag="after_windows")
+                nc.scalar.activation(squares[:, 0], diff[:], ACT.Square, scale=DIFF_SCALE)
+                nc.scalar.activation(squares[:, 1], mean[:], ACT.Square, scale=FETCH)
                 total = keep.tile([P, 2, HALF], F32, name="total")
-                nc.vector.tensor_tensor(total[:], diff_sq[:], mean_sq[:], ALU.add)
+                nc.vector.tensor_tensor(total[:], squares[:, 0], squares[:, 1], ALU.add)
                 for n, t in enumerate(tiles):
-                    nc.scalar.activation(
-                        inv_root[h][:, t, :],
-                        total[:, n, :],
-                        ACT.Abs_reciprocal_sqrt,
-                        bias=0.1,
-                        scale=gn_inv_sq[:, t : t + 1],
-                    )
-                continue
-
-            blocks = [(t, slice(k * P, (k + 1) * P)) for t in tiles for k in range(HALF // P)]
-            diff_t = bank([P, 4, P], "turned%d" % min(step, 1))
-            for n, (t, cols) in enumerate(blocks):
-                add_turned(diff_t[:, n, :], a_neg[:, t, cols], b_pos[:, t, cols])
-            diff_sq = keep.tile([P, 4, P], F32, name="diff_sq%d" % step, tag="diff_sq%d" % step)
-            nc.scalar.activation(diff_sq[:], diff_t[:], ACT.Square, scale=1.6)
-            mean_t = bank([P, 4, P], "turned%d" % (1 - min(step, 1)))
-            for n, (t, cols) in enumerate(blocks):
-                add_turned(mean_t[:, n, :], win[t][:, h * HALF : (h + 1) * HALF][:, cols], both[h][:, t, cols])
-            mean_sq = keep.tile([P, 4, P], F32, name="mean_sq%d" % step, tag="mean_sq%d" % step, align_bytes=64)
-            nc.scalar.activation(mean_sq[:], mean_t[:], ACT.Square, scale=0.6)
-            spread = bank([P, 4, P], "spread%d" % (step % 2))
-            for n in range(4):
-                add_turned(spread[:, n, :], diff_sq[:, n, :], mean_sq[:, n, :])
-            for n, t in enumerate(tiles):
-                nc.scalar.activation(
-                    inv_root[h][:, t, :],
-                    spread[:, 2 * n : 2 * n + 2, :].rearrange("p k j -> p (k j)"),
-                    ACT.Abs_reciprocal_sqrt,
-                    bias=0.1,
-                    scale=gn_inv_sq[:, t : t + 1],
-                )
+                    inverse_root(h, t, total[:, n, :])
+            else:
+                blocks = [(n, t, slice(k * P, (k + 1) * P)) for n, t in enumerate(tiles) for k in range(HALF // P)]
+                diff_bank = min(step, 1)
+                diff_t = bank([P, len(blocks), P], "turned%d" % diff_bank)
+                for b, (n, t, cols) in enumerate(blocks):
+                    add_turned(diff_t[:, b, :], a_neg[:, n, cols], b_pos[:, n, cols])
+                diff_sq = keep.tile([P, len(blocks), P], F32, name="diff_sq%d" % step)
+                nc.scalar.activation(diff_sq[:], diff_t[:], ACT.Square, scale=DIFF_SCALE)
+                mean_t = bank([P, len(blocks), P], "turned%d" % (1 - diff_bank))
+                for b, (n, t, cols) in enumerate(blocks):
+                    add_turned(mean_t[:, b, :], win[t][:, halves[h]][:, cols], both[h][:, t, cols])
+                mean_sq = keep.tile([P, len(blocks), P], F32, name="mean_sq%d" % step)
+                nc.scalar.activation(mean_sq[:], mean_t[:], ACT.Square, scale=FETCH)
+                spread = bank([P, len(blocks), P], "spread%d" % (step % 2))
+                for b in range(len(blocks)):
+                    add_turned(spread[:, b, :], diff_sq[:, b, :], mean_sq[:, b, :])
+                for n, t in enumerate(tiles):
+                    inverse_root(h, t, spread[:, 2 * n : 2 * n + 2, :].rearrange("p k j -> p (k j)"))
 
             if step == 0:
                 w_bf = keep.tile([P, N, PACK], BF16, name="w_bf", align_bytes=64)
@@ -206,21 +208,20 @@ def tile_picked_scorestd_none_p_kernel(
         )
 
         out_view = out.rearrange("(mb p) j -> p mb j", p=P)
-        result_banks = ["product0", "product1", "product2", "product3", "spread0", "turned0"]
-        for piece, (start, width) in enumerate(((0, 256), (256, 128), (384, 128))):
+        result_banks = ["turned0", "spread0", "product0", "product1", "product2", "product3"]
+        for piece, (start, width) in enumerate(PIECES):
             h, inside = divmod(start, HALF)
             if inside == 0:
-                num = keep.tile([P, PACK, HALF], F32, name="num", tag="num")
+                numerator = keep.tile([P, PACK, HALF], F32, name="numerator", tag="numerator")
                 for t in range(PACK):
                     nc.vector.scalar_tensor_tensor(
-                        num[:, t, :], win[t][:, start : start + HALF], 1.32, both[h][:, t, :], ALU.mult, ALU.add
+                        numerator[:, t, :], win[t][:, halves[h]], NUM_W, both[h][:, t, :], ALU.mult, ALU.add
                     )
             part = slice(inside, inside + width)
-            z_tag = "mean_sq1" if piece == 0 else "z%d" % piece
-            z = keep.tile([P, width, PACK], BF16, name="z%d" % piece, tag=z_tag, align_bytes=64)
+            z = keep.tile([P, width, PACK], BF16, name="z%d" % piece, align_bytes=64)
             nc.vector.tensor_tensor(
                 z[:].rearrange("p (c i) t -> p c t i", i=4),
-                num[:, :, part].rearrange("p t (c i) -> p c t i", i=4),
+                numerator[:, :, part].rearrange("p t (c i) -> p c t i", i=4),
                 inv_root[h][:, :, part].rearrange("p t (c i) -> p c t i", i=4),
                 ALU.mult,
             )
@@ -243,7 +244,7 @@ def tile_picked_scorestd_none_p_kernel(
                         stop=True,
                     )
                 staged_out = keep.tile([P, 2, width], F32, name="staged_out%d_%d" % (piece, side))
-                if piece == 2 and side == 1:
+                if piece > 0 and side == 1:
                     nc.vector.tensor_copy(staged_out[:], result[:])
                 else:
                     nc.scalar.copy(staged_out[:], result[:])

from contextlib import ExitStack

import concourse.mybir as mybir
from concourse.masks import make_identity

F32 = mybir.dt.float32
BF16 = mybir.dt.bfloat16
I32 = mybir.dt.int32
U32 = mybir.dt.uint32
U16 = mybir.dt.uint16
U8 = mybir.dt.uint8
FP8X4 = mybir.dt.float8_e4m3fn_x4
ALU = mybir.AluOpType
ACT = mybir.ActivationFunctionType

P = 128
PACK = 4
K = 512
TABLE = 2048
H = 512
S = 512
N = 512
HALF = S // 2
LIST_ROWS = 16
QUADRANT = 32
BLOCK_ROWS = 8
FLOPS = 2 * K * H * S + 2 * H * N * S

SCORE = 0.0625
MEAN = 0.3125
EPS = 0.1
FETCH = (1 - 2 * MEAN) / (2 * MEAN)
NUM_W = (1 - MEAN) * FETCH / MEAN
DIFF_SCALE = 0.5 / MEAN
TINY = 1e-30

STEPS = 4
LAST_STEP = STEPS - 1
PIECES = ((0, 256), (256, 128), (384, 128))


def tile_picked_scorestd_none_p_kernel(
    tc, x_words, x_scales, d_words, d_scales, gn, w1, offs, kidx, n1, n2, out
):
    nc = tc.nc
    with ExitStack() as ctx:
        keep = ctx.enter_context(tc.tile_pool(name="keep", bufs=1))
        psum = ctx.enter_context(tc.psum_pool(name="psum", bufs=1))

        def bank(shape, tag):
            return psum.tile(shape, F32, name=tag, tag=tag)

        kidx_sb = keep.tile([P, H // LIST_ROWS], U16, name="kidx_sb")
        offs_sb = keep.tile([P, S // LIST_ROWS], U16, name="offs_sb")
        n1_sb = keep.tile([P, S // LIST_ROWS], U16, name="n1_sb")
        n2_sb = keep.tile([P, S // LIST_ROWS], U16, name="n2_sb")
        d_bytes = keep.tile([P, TABLE], U8, name="d_bytes")
        x_bytes = keep.tile([P, TABLE], U8, name="x_bytes")
        d_table = keep.tile([P, TABLE], U32, name="d_table")
        x_table = keep.tile([P, TABLE], U32, name="x_table", tag="after_x")
        gn_sb = keep.tile([P, PACK], F32, name="gn_sb")

        nc.gpsimd.memset(d_bytes[:].bitcast(I32), 0)
        nc.vector.memset(x_bytes[:].bitcast(I32), 0)
        nc.sync.dma_start(kidx_sb[:], kidx)
        nc.sync.dma_start(out=d_bytes[0:P:BLOCK_ROWS, :].bitcast(I32), in_=d_scales[0].bitcast(I32))
        nc.sync.dma_start(offs_sb[:], offs)
        nc.sync.dma_start(out=x_bytes[0:P:BLOCK_ROWS, :].bitcast(I32), in_=x_scales[0].bitcast(I32))
        nc.scalar.dma_start(out=gn_sb[:], in_=gn.rearrange("(p t) o -> p (t o)", t=PACK))
        nc.sync.dma_start(out=d_table[:].bitcast(I32), in_=d_words[0].rearrange("p n t -> p (n t)").bitcast(I32))
        nc.sync.dma_start(out=x_table[:].bitcast(I32), in_=x_words[0].rearrange("p n t -> p (n t)").bitcast(I32))
        nc.sync.dma_start(n1_sb[:], n1)
        nc.sync.dma_start(n2_sb[:], n2)

        planes = keep.tile([P, H + S], U8, name="planes", align_bytes=64)
        nc.vector.memset(planes[:].bitcast(I32), 0)
        d_bytes_picked = keep.tile([P, H], U8, name="d_bytes_picked")
        x_bytes_picked = keep.tile([P, S], U8, name="x_bytes_picked")
        staged = keep.tile([P, H + S], U8, name="staged")
        nc.vector.tensor_copy(d_bytes_picked[:], d_bytes[:].indirect(kidx_sb[:]))
        nc.vector.tensor_copy(x_bytes_picked[:], x_bytes[:].indirect(offs_sb[:]))
        nc.vector.tensor_copy(
            staged[:, 0:H].rearrange("p (t g i) -> p g t i", t=PACK, i=16),
            d_bytes_picked[:].rearrange("p (g i t) -> p g t i", t=PACK, i=16),
        )
        nc.vector.tensor_copy(staged[:, H : H + S].bitcast(I32), x_bytes_picked[:].bitcast(I32))
        for r in range(QUADRANT // BLOCK_ROWS):
            nc.scalar.dma_start(
                out=planes[r:P:QUADRANT, :].bitcast(I32), in_=staged[BLOCK_ROWS * r : P : QUADRANT, :].bitcast(I32)
            )

        d_picked = keep.tile([P, H], U32, name="d_picked")
        d_dealt = keep.tile([P, H], U32, name="d_dealt", align_bytes=64)
        nc.vector.tensor_copy(d_picked[:], d_table[:].indirect(kidx_sb[:]))
        nc.vector.tensor_copy(
            d_dealt[:].rearrange("p (t g i) -> p g t i", t=PACK, i=4),
            d_picked[:].rearrange("p (g i t) -> p g t i", t=PACK, i=4),
        )

        row_scale = keep.tile([P, PACK], F32, name="row_scale", tag="after_windows")
        gn_sq = keep.tile([P, PACK], F32, name="gn_sq")
        gn_inv = keep.tile([P, PACK], F32, name="gn_inv")
        gn_inv_sq = keep.tile([P, PACK], F32, name="gn_inv_sq")
        nc.scalar.activation(row_scale[:], gn_sb[:], ACT.Copy, scale=SCORE * MEAN / FETCH)
        nc.scalar.activation(gn_sq[:], gn_sb[:], ACT.Square)
        nc.scalar.activation(gn_inv[:], gn_sq[:], ACT.Abs_reciprocal_sqrt, bias=TINY)
        nc.scalar.activation(gn_inv_sq[:], gn_inv[:], ACT.Square)

        x_picked = keep.tile([P, S], U32, name="x_picked", align_bytes=64)
        win = [keep.tile([P, S], F32, name="win%d" % t) for t in range(PACK)]
        halves = [slice(h * HALF, (h + 1) * HALF) for h in range(2)]
        entries = [slice(h * HALF // LIST_ROWS, (h + 1) * HALF // LIST_ROWS) for h in range(2)]
        for h in range(2):
            nc.vector.tensor_copy(x_picked[:, halves[h]], x_table[:].indirect(offs_sb[:, entries[h]]))

        w_raw = keep.tile([P, PACK, N], F32, name="w_raw", tag="after_x")
        nc.sync.dma_start(out=w_raw[:], in_=w1.rearrange("(p t) m -> p t m", t=PACK))

        for t in range(PACK):
            keys = slice(t * P, (t + 1) * P)
            for n, cols in enumerate(halves if t < 2 else [slice(0, S)]):
                scores = bank([P, cols.stop - cols.start], ("product%d" if n == 0 else "turned%d") % t)
                nc.tensor.matmul_mx(
                    out=scores[:],
                    lhsT=d_dealt[:, keys].bitcast(FP8X4),
                    lhsT_scale=planes[:, keys],
                    rhs=x_picked[:, cols].bitcast(FP8X4),
                    rhs_scale=planes[:, H + cols.start : H + cols.stop],
                    start=True,
                    stop=True,
                )
                nc.scalar.activation(win[t][:, cols], scores[:], ACT.Copy, scale=row_scale[:, t : t + 1])

        ident = keep.tile([P, P], F32, name="ident")
        make_identity(nc, ident[:])

        def add_turned(dst, first, second):
            nc.tensor.matmul(dst, first, ident[:], start=True, stop=False, is_transpose=True)
            nc.tensor.matmul(dst, second, ident[:], start=False, stop=True, is_transpose=True)

        def inverse_root(h, t, total):
            nc.scalar.activation(
                inv_root[h][:, t, :], total, ACT.Abs_reciprocal_sqrt, bias=EPS, scale=gn_inv_sq[:, t : t + 1]
            )

        both = [keep.tile([P, PACK, HALF], F32, name="both%d" % h) for h in range(2)]
        inv_root = [keep.tile([P, PACK, HALF], F32, name="inv_root%d" % h) for h in range(2)]
        fetched_tags = ["fetched0", "fetched1", "after_windows", "fetched0"]
        for step in range(STEPS):
            h, pair = divmod(step, 2)
            tiles = (2 * pair, 2 * pair + 1)
            fetched = keep.tile([P, 2, 2, HALF], F32, name="fetched%d" % step, tag=fetched_tags[step])
            a_neg = fetched[:, 0]
            b_pos = fetched[:, 1]
            for n, t in enumerate(tiles):
                from_n1 = win[t][:].indirect(n1_sb[:, entries[h]])
                from_n2 = win[t][:].indirect(n2_sb[:, entries[h]])
                nc.vector.tensor_scalar(a_neg[:, n, :], from_n1, -FETCH, 0.0, ALU.mult, ALU.add)
                nc.vector.tensor_scalar(b_pos[:, n, :], from_n2, FETCH, 0.0, ALU.mult, ALU.add)
            adder = nc.vector if step == LAST_STEP else nc.gpsimd
            adder.tensor_tensor(both[h][:, 2 * pair : 2 * pair + 2, :], a_neg, b_pos, ALU.subtract)

            if step == LAST_STEP:
                diff = keep.tile([P, 2, HALF], F32, name="diff")
                nc.vector.tensor_tensor(diff[:], a_neg, b_pos, ALU.add)
                mean = keep.tile([P, 2, HALF], F32, name="mean")
                for n, t in enumerate(tiles):
                    nc.vector.tensor_tensor(mean[:, n, :], win[t][:, halves[h]], both[h][:, t, :], ALU.add)
                squares = keep.tile([P, 2, 2, HALF], F32, name="squares", tag="after_windows")
                nc.scalar.activation(squares[:, 0], diff[:], ACT.Square, scale=DIFF_SCALE)
                nc.scalar.activation(squares[:, 1], mean[:], ACT.Square, scale=FETCH)
                total = keep.tile([P, 2, HALF], F32, name="total")
                nc.vector.tensor_tensor(total[:], squares[:, 0], squares[:, 1], ALU.add)
                for n, t in enumerate(tiles):
                    inverse_root(h, t, total[:, n, :])
            else:
                blocks = [(n, t, slice(k * P, (k + 1) * P)) for n, t in enumerate(tiles) for k in range(HALF // P)]
                diff_bank = min(step, 1)
                diff_t = bank([P, len(blocks), P], "turned%d" % diff_bank)
                for b, (n, t, cols) in enumerate(blocks):
                    add_turned(diff_t[:, b, :], a_neg[:, n, cols], b_pos[:, n, cols])
                diff_sq = keep.tile([P, len(blocks), P], F32, name="diff_sq%d" % step)
                nc.scalar.activation(diff_sq[:], diff_t[:], ACT.Square, scale=DIFF_SCALE)
                mean_t = bank([P, len(blocks), P], "turned%d" % (1 - diff_bank))
                for b, (n, t, cols) in enumerate(blocks):
                    add_turned(mean_t[:, b, :], win[t][:, halves[h]][:, cols], both[h][:, t, cols])
                mean_sq = keep.tile([P, len(blocks), P], F32, name="mean_sq%d" % step)
                nc.scalar.activation(mean_sq[:], mean_t[:], ACT.Square, scale=FETCH)
                spread = bank([P, len(blocks), P], "spread%d" % (step % 2))
                for b in range(len(blocks)):
                    add_turned(spread[:, b, :], diff_sq[:, b, :], mean_sq[:, b, :])
                for n, t in enumerate(tiles):
                    inverse_root(h, t, spread[:, 2 * n : 2 * n + 2, :].rearrange("p k j -> p (k j)"))

            if step == 0:
                w_bf = keep.tile([P, N, PACK], BF16, name="w_bf", align_bytes=64)
                for mb in range(N // P):
                    rows = slice(mb * P, (mb + 1) * P)
                    nc.scalar.copy(
                        w_bf[:, rows, :].rearrange("p (c i) t -> p c t i", i=4),
                        w_raw[:, :, rows].rearrange("p t (c i) -> p c t i", i=4),
                    )

        w_codes = keep.tile([P, N], U32, name="w_codes", align_bytes=64)
        w_plane = keep.tile([P, N], U8, name="w_plane", align_bytes=64)
        nc.vector.quantize_mx(
            out=w_codes[:].bitcast(FP8X4), scales=w_plane[:], in_=w_bf[:].rearrange("p m t -> p (m t)")
        )

        out_view = out.rearrange("(mb p) j -> p mb j", p=P)
        result_banks = ["turned0", "spread0", "product0", "product1", "product2", "product3"]
        for piece, (start, width) in enumerate(PIECES):
            h, inside = divmod(start, HALF)
            if inside == 0:
                numerator = keep.tile([P, PACK, HALF], F32, name="numerator", tag="numerator")
                for t in range(PACK):
                    nc.vector.scalar_tensor_tensor(
                        numerator[:, t, :], win[t][:, halves[h]], NUM_W, both[h][:, t, :], ALU.mult, ALU.add
                    )
            part = slice(inside, inside + width)
            z = keep.tile([P, width, PACK], BF16, name="z%d" % piece, align_bytes=64)
            nc.vector.tensor_tensor(
                z[:].rearrange("p (c i) t -> p c t i", i=4),
                numerator[:, :, part].rearrange("p t (c i) -> p c t i", i=4),
                inv_root[h][:, :, part].rearrange("p t (c i) -> p c t i", i=4),
                ALU.mult,
            )
            z_codes = keep.tile([P, width], U32, name="z_codes%d" % piece, align_bytes=64)
            z_plane = keep.tile([P, width], U8, name="z_plane%d" % piece, align_bytes=64)
            nc.vector.quantize_mx(
                out=z_codes[:].bitcast(FP8X4), scales=z_plane[:], in_=z[:].rearrange("p j t -> p (j t)")
            )
            for side in range(2):
                result = bank([P, 2, width], result_banks[2 * piece + side])
                for n in range(2):
                    rows = slice((2 * side + n) * P, (2 * side + n + 1) * P)
                    nc.tensor.matmul_mx(
                        out=result[:, n, :],
                        lhsT=w_codes[:, rows].bitcast(FP8X4),
                        lhsT_scale=w_plane[:, rows],
                        rhs=z_codes[:].bitcast(FP8X4),
                        rhs_scale=z_plane[:],
                        start=True,
                        stop=True,
                    )
                staged_out = keep.tile([P, 2, width], F32, name="staged_out%d_%d" % (piece, side))
                if piece > 0 and side == 1:
                    nc.vector.tensor_copy(staged_out[:], result[:])
                else:
                    nc.scalar.copy(staged_out[:], result[:])
                nc.sync.dma_start(out=out_view[:, 2 * side : 2 * side + 2, start : start + width], in_=staged_out[:])
